import numpy as np
import ml_dtypes


def mxq(x, axis, fmt="e4m3"):
    dtype, down = {"e4m3": (ml_dtypes.float8_e4m3fn, 7), "e5m2": (ml_dtypes.float8_e5m2, 14)}[fmt]
    v = np.moveaxis(np.asarray(x, np.float32).astype(ml_dtypes.bfloat16).astype(np.float64), axis, -1)
    blocks = v.reshape(v.shape[:-1] + (-1, 32))
    amax = np.abs(blocks).max(-1, keepdims=True)
    byte = np.maximum(np.where(amax > 0, np.frexp(amax)[1] - 1 + 127, 0) - down, 1)
    scale = np.exp2(byte - 127.0)
    codes = (blocks / scale).astype(np.float32).astype(dtype).astype(np.float64)
    return np.moveaxis((codes * scale).reshape(v.shape), -1, axis)


WIDE = False


def mx_kscale(k):
    if not WIDE:
        return np.ones(k)
    levels = np.array([10, -10, 5, -5, 0])
    if k % 512:
        return np.exp2(np.random.permutation(np.resize(levels, k // 32))).repeat(32)
    a = np.empty((k // 512, 16))
    for p in range(k // 512):
        a[p, :8] = np.random.permutation(np.resize(levels, 8))
        for g in range(8):
            far = levels[np.abs(levels - a[p, g]) >= 10]
            a[p, g + 8] = far[np.random.randint(len(far))]
    return np.exp2(a.ravel()).repeat(32)


def f64(x):
    return np.asarray(x).astype(np.float64)


def striped(idx):
    return np.tile(idx.reshape(-1, 16).T, (8, 1)).astype(np.uint16)


def unstriped(offs):
    return offs[:16].T.reshape(-1).astype(np.int64)


E2M1 = np.array([0.0, 0.5, 1.0, 1.5, 2.0, 3.0, 4.0, 6.0, -0.0, -0.5, -1.0, -1.5, -2.0, -3.0, -4.0, -6.0])


def pack_weight(w, fmt):
    k, n = w.shape
    w = f64(np.asarray(w, np.float32).astype(ml_dtypes.bfloat16)).reshape(k // 32, 32, n)
    amax = np.abs(w).max(1)
    if fmt == "e4m3":
        byte = np.frexp(amax)[1] - 1 + 127 - 7
    else:
        mant, ex = np.frexp(amax / 6.0)
        byte = np.where(mant > 0.5, ex, ex - 1) + 127
    byte = np.clip(np.where(amax > 0, byte, 1), 1, 254)
    scaled = (w * np.exp2(127.0 - byte)[:, None, :]).reshape(k, n).astype(np.float32)
    by_word = np.ascontiguousarray(scaled.reshape(k // 512, 128, 4, n).transpose(0, 1, 3, 2))
    if fmt == "e4m3":
        words = by_word.astype(ml_dtypes.float8_e4m3fn).view(np.uint8)
    else:
        c = by_word.astype(ml_dtypes.float4_e2m1fn).view(np.uint8) & 0xF
        words = (c[..., 0::2] | (c[..., 1::2] << 4)).reshape(k // 512, 128, 2 * n)
    return np.ascontiguousarray(words), np.ascontiguousarray(byte.astype(np.uint8).reshape(k // 512, 16, n))


def unpack_weight(words, scales, fmt):
    g, _, n = scales.shape
    words = np.ascontiguousarray(words).reshape(g, 128, n, -1)
    if fmt == "e4m3":
        vals = words.view(ml_dtypes.float8_e4m3fn).astype(np.float64)
    else:
        nib = np.empty((g, 128, n, 4), np.uint8)
        nib[..., 0::2] = words & 0xF
        nib[..., 1::2] = words >> 4
        vals = E2M1[nib]
    vals = vals * np.repeat(np.exp2(scales.astype(np.float64) - 127.0), 8, axis=1)[..., None]
    return vals.transpose(0, 1, 3, 2).reshape(g * 512, n)


def relu2(v):
    return np.maximum(v, 0.0) ** 2


K, T, E, C, N = 2560, 512, 2, 256, 384


def by_expert(wq, xq):
    return np.concatenate([wq[e].T @ xq[:, e * C:(e + 1) * C] for e in range(E)], axis=1)


def setup_inputs():
    n = np.random.standard_normal
    s = mx_kscale(K)[:, None]
    w = [pack_weight(m, "e2m1") for m in n((E, K, N)) / np.sqrt(K) / s[None]]
    return {
        "xT": (n((K, T)) * s).astype(np.float32),
        "w_words": np.stack([m[0] for m in w]),
        "w_scales": np.stack([m[1] for m in w]),
        "b": (0.3 * n((N, E))).astype(np.float32),
        "gate": np.tile(np.random.uniform(0.2, 1.0, E * C), (K, 1)).astype(np.float32),
        "offs": striped(np.random.permutation(T)[:E * C]),
    }


def reference(xT, w_words, w_scales, b, gate, offs):
    idx = unstriped(offs)
    w = np.stack([unpack_weight(w_words[e], w_scales[e], "e2m1") for e in range(E)])
    xq = mxq(f64(gate) * f64(xT)[:, idx], 0, "e4m3")
    y = by_expert(w, xq)
    y = relu2(y + np.repeat(f64(b), C, axis=1))
    out = np.zeros((N, T))
    out[:, idx] = y
    return out

@@ -1,0 +1,193 @@
+from contextlib import ExitStack
+
+import concourse.mybir as mybir
+
+K, T, E, C, N = 2560, 512, 2, 256, 384
+FLOPS = 2 * K * N * E * C
+BYTES = K * T * 4 + E * K * N // 2 + E * K // 32 * N + N * E * 4 + E * C * 4 + 128 * 32 * 2 + N * T * 4
+
+F32 = mybir.dt.float32
+BF16 = mybir.dt.bfloat16
+I32 = mybir.dt.int32
+U32 = mybir.dt.uint32
+U16 = mybir.dt.uint16
+U8 = mybir.dt.uint8
+FP8X4 = mybir.dt.float8_e4m3fn_x4
+FP4X4 = mybir.dt.float4_e2m1fn_x4
+MULT = mybir.AluOpType.mult
+COPY = mybir.ActivationFunctionType.Copy
+RELU = mybir.ActivationFunctionType.Relu
+
+P = 128
+PACK = 4
+PASSES = K // (P * PACK)
+BLOCKS = N // P
+HALF = 128
+HALVES = C // HALF
+SPARE = 8
+JOINT = 3
+BANKS = 8
+
+
+def tile_moe_pre_lin_relu2_kernel(tc, xT, w_words, w_scales, b, gate, offs, out):
+    nc = tc.nc
+    with ExitStack() as ctx:
+        keep = ctx.enter_context(tc.tile_pool(name="keep", bufs=1))
+        psum = ctx.enter_context(tc.psum_pool(name="psum", bufs=1))
+
+        def new(shape, dtype, name, tag=None):
+            return keep.tile(shape, dtype, name=name, tag=tag or name, align_bytes=64)
+
+        offsets = keep.tile([P, E * C // 16], U16, name="offsets")
+        gates = new([P, E * C], F32, "gates")
+        planes = {}
+        for a in range(PASSES):
+            for t in range(PACK):
+                planes[a, t] = new([P, T + (SPARE if a < JOINT else 0)], F32, f"x{a}{t}")
+        w_codes = [new([P, PASSES, 2 * N], U8, f"w{e}") for e in range(E)]
+        w_plane = new([P, E * PASSES * N], U8, "w_plane")
+        bias = new([P, BLOCKS, E], F32, "bias")
+
+        for a in range(JOINT):
+            for t in range(PACK):
+                nc.vector.memset(planes[a, t][:, T:], 0.0)
+        nc.vector.memset(w_plane[:].bitcast(I32), 0)
+
+        rows = xT.rearrange("(a p t) s -> a t p s", p=P, t=PACK)
+
+        def load_x(a):
+            for t in range(PACK):
+                nc.sync.dma_start(planes[a, t][:, :T], rows[a, t])
+
+        nc.sync.dma_start(offsets[:], offs)
+        nc.sync.dma_start(gates[:, :C], gate[:P, :C])
+        nc.sync.dma_start(planes[0, 0][:, :T], rows[0, 0])
+        nc.sync.dma_start(gates[:, C:], gate[:P, C:])
+        for t in range(1, PACK):
+            nc.sync.dma_start(planes[0, t][:, :T], rows[0, t])
+        load_x(1)
+        nc.sync.dma_start(bias[:], b.rearrange("(c p) e -> p c e", p=P))
+        load_x(2)
+        scale_rows = w_scales.rearrange("e a (q r) n -> r q (e a) n", r=4)
+        for r in range(4):
+            nc.sync.dma_start(
+                w_plane[:].bitcast(I32)[r:P:32, :].rearrange("q (g n) -> q g n", g=E * PASSES),
+                scale_rows[r].bitcast(I32),
+            )
+        for e in range(E):
+            nc.sync.dma_start(w_codes[e][:].bitcast(I32), w_words[e].rearrange("a p n -> p a n").bitcast(I32))
+        load_x(3)
+        load_x(4)
+
+        bias0 = new([P, BLOCKS], F32, "bias0", tag="first_bias")
+        nc.scalar.activation(bias0[:], bias[:, :, 0], COPY)
+
+        gathered, rounded, codes, scales, acc, relu, outs = {}, {}, {}, {}, {}, {}, {}
+
+        def gather(a, experts, tag):
+            lo, hi = experts[0] * C, (experts[-1] + 1) * C
+            g = new([P, PACK, hi - lo], F32, f"g{a}{experts[0]}", tag)
+            for t in range(PACK):
+                cuts = [lo, lo + C, hi] if (a, t) == (0, 0) else [lo, hi]
+                for s0, s1 in zip(cuts, cuts[1:]):
+                    nc.vector.tensor_tensor(
+                        g[:, t, s0 - lo : s1 - lo],
+                        planes[a, t][:].indirect(offsets[:, s0 // 16 : s1 // 16]),
+                        gates[:, s0:s1],
+                        MULT,
+                    )
+            for e in experts:
+                gathered[a, e] = g[:, :, e * C - lo : (e + 1) * C - lo]
+
+        def interleave(a, e, tag=None):
+            rounded[a, e] = new([P, C, PACK], BF16, f"r{a}{e}", tag)
+            nc.scalar.activation(
+                rounded[a, e][:].rearrange("p (c i) t -> p c t i", i=4),
+                gathered[a, e].rearrange("p t (c i) -> p c t i", i=4),
+                COPY,
+            )
+
+        def quantize(a, e, tag=None):
+            codes[a, e] = new([P, C], U32, f"c{a}{e}", tag)
+            scales[a, e] = new([P, C], U8, f"s{a}{e}")
+            nc.vector.quantize_mx(
+                out=codes[a, e][:].bitcast(FP8X4),
+                scales=scales[a, e][:],
+                in_=rounded[a, e][:].rearrange("p c t -> p (c t)"),
+            )
+
+        def multiply(a, e, blocks):
+            for blk in blocks:
+                for h in range(HALVES):
+                    if a == 0:
+                        bank = ((e * BLOCKS + blk) * HALVES + h) % BANKS
+                        acc[e, blk, h] = psum.tile([P, HALF], F32, name=f"acc{e}{blk}{h}", tag=f"bank{bank}")
+                    col = (e * PASSES + a) * N + blk * P
+                    nc.tensor.matmul_mx(
+                        out=acc[e, blk, h][:],
+                        lhsT=w_codes[e][:, a, 2 * blk * P : 2 * (blk + 1) * P].bitcast(FP4X4),
+                        lhsT_scale=w_plane[:, col : col + P],
+                        rhs=codes[a, e][:, h * HALF : (h + 1) * HALF].bitcast(FP8X4),
+                        rhs_scale=scales[a, e][:, h * HALF : (h + 1) * HALF],
+                        start=(a == 0),
+                        stop=(a == PASSES - 1),
+                    )
+
+        def rectify(e, blk):
+            relu[e, blk] = new([P, C], F32, f"y{e}{blk}")
+            col = bias0[:, blk : blk + 1] if e == 0 else bias[:, blk, 1:2]
+            for h in range(HALVES):
+                nc.scalar.activation(relu[e, blk][:, h * HALF : (h + 1) * HALF], acc[e, blk, h][:], RELU, bias=col)
+
+        def scatter(e, blk, tag=None):
+            if e == 0:
+                outs[blk] = new([P, T], F32, f"o{blk}", tag)
+            y = relu[e, blk][:]
+            nc.vector.tensor_tensor(outs[blk][:].indirect(offsets[:, e * C // 16 : (e + 1) * C // 16]), y, y, MULT)
+
+        every, early, late = range(BLOCKS), [0], [1, 2]
+
+        def finish(a, e, tag=None):
+            quantize(a, e, tag)
+            multiply(a, e, every if e == 0 else early)
+
+        gather(0, [0, 1], None)
+        interleave(0, 0)
+        interleave(0, 1)
+        gather(1, [0, 1], None)
+        interleave(1, 0)
+        interleave(1, 1)
+        finish(0, 0)
+        finish(0, 1)
+        gather(2, [0, 1], "r01")
+        interleave(2, 0)
+        interleave(2, 1)
+        finish(1, 0)
+        finish(1, 1)
+        gather(3, [0], "r11")
+        interleave(3, 0)
+        finish(2, 0)
+        gather(4, [0], "r20")
+        interleave(4, 0)
+        finish(2, 1)
+        finish(3, 0)
+        gather(3, [1], "r30")
+        interleave(3, 1)
+        finish(4, 0)
+        gather(4, [1], "r40")
+        for blk in every:
+            rectify(0, blk)
+        interleave(4, 1, "first_bias")
+        for a in range(3):
+            multiply(a, 1, late)
+        quantize(3, 1)
+        multiply(3, 1, every)
+        scatter(0, 0)
+        quantize(4, 1, "y00")
+        multiply(4, 1, every)
+        scatter(0, 1, "first_bias")
+        scatter(0, 2, "y01")
+        for blk in every:
+            rectify(1, blk)
+            scatter(1, blk)
+            nc.sync.dma_start(out[blk * P : (blk + 1) * P, :], outs[blk][:])

@@ -17,6 +17,7 @@ FP4X4 = mybir.dt.float4_e2m1fn_x4
 MULT = mybir.AluOpType.mult
 COPY = mybir.ActivationFunctionType.Copy
 RELU = mybir.ActivationFunctionType.Relu
+SQUARE = mybir.ActivationFunctionType.Square
 
 P = 128
 PACK = 4
@@ -25,7 +26,7 @@ BLOCKS = N // P
 HALF = 128
 HALVES = C // HALF
 SPARE = 8
-JOINT = 3
+JOINT = 2
 BANKS = 8
 
 
@@ -82,7 +83,7 @@ def tile_moe_pre_lin_relu2_kernel(tc, xT, w_words, w_scales, b, gate, offs, out)
         bias0 = new([P, BLOCKS], F32, "bias0", tag="first_bias")
         nc.scalar.activation(bias0[:], bias[:, :, 0], COPY)
 
-        gathered, rounded, codes, scales, acc, relu, outs = {}, {}, {}, {}, {}, {}, {}
+        gathered, rounded, codes, scales, acc, relu, squared, outs = {}, {}, {}, {}, {}, {}, {}, {}
 
         def gather(a, experts, tag):
             lo, hi = experts[0] * C, (experts[-1] + 1) * C
@@ -96,25 +97,25 @@ def tile_moe_pre_lin_relu2_kernel(tc, xT, w_words, w_scales, b, gate, offs, out)
                         gates[:, s0:s1],
                         MULT,
                     )
-            for e in experts:
-                gathered[a, e] = g[:, :, e * C - lo : (e + 1) * C - lo]
+            gathered[a, experts[0]] = g
 
-        def interleave(a, e, tag=None):
-            rounded[a, e] = new([P, C, PACK], BF16, f"r{a}{e}", tag)
+        def interleave(a, experts, tag=None):
+            g = gathered[a, experts[0]]
+            r = new([P, len(experts) * C, PACK], BF16, f"r{a}{experts[0]}", tag)
             nc.scalar.activation(
-                rounded[a, e][:].rearrange("p (c i) t -> p c t i", i=4),
-                gathered[a, e].rearrange("p t (c i) -> p c t i", i=4),
-                COPY,
+                r[:].rearrange("p (c i) t -> p c t i", i=4), g[:].rearrange("p t (c i) -> p c t i", i=4), COPY
             )
+            rounded[a, experts[0]] = r
 
-        def quantize(a, e, tag=None):
-            codes[a, e] = new([P, C], U32, f"c{a}{e}", tag)
-            scales[a, e] = new([P, C], U8, f"s{a}{e}")
+        def quantize(a, experts):
+            c = new([P, len(experts) * C], U32, f"c{a}{experts[0]}")
+            s = new([P, len(experts) * C], U8, f"s{a}{experts[0]}")
             nc.vector.quantize_mx(
-                out=codes[a, e][:].bitcast(FP8X4),
-                scales=scales[a, e][:],
-                in_=rounded[a, e][:].rearrange("p c t -> p (c t)"),
+                out=c[:].bitcast(FP8X4), scales=s[:], in_=rounded[a, experts[0]][:].rearrange("p c t -> p (c t)")
             )
+            for i, e in enumerate(experts):
+                codes[a, e] = c[:, i * C : (i + 1) * C]
+                scales[a, e] = s[:, i * C : (i + 1) * C]
 
         def multiply(a, e, blocks):
             for blk in blocks:
@@ -139,55 +140,47 @@ def tile_moe_pre_lin_relu2_kernel(tc, xT, w_words, w_scales, b, gate, offs, out)
             for h in range(HALVES):
                 nc.scalar.activation(relu[e, blk][:, h * HALF : (h + 1) * HALF], acc[e, blk, h][:], RELU, bias=col)
 
+        def square(e, blk, tag=None):
+            squared[e, blk] = new([P, C], F32, f"z{e}{blk}", tag)
+            nc.scalar.activation(squared[e, blk][:], relu[e, blk][:], SQUARE)
+
         def scatter(e, blk, tag=None):
             if e == 0:
                 outs[blk] = new([P, T], F32, f"o{blk}", tag)
-            y = relu[e, blk][:]
-            nc.vector.tensor_tensor(outs[blk][:].indirect(offsets[:, e * C // 16 : (e + 1) * C // 16]), y, y, MULT)
+            nc.vector.tensor_copy(
+                outs[blk][:].indirect(offsets[:, e * C // 16 : (e + 1) * C // 16]), squared[e, blk][:]
+            )
 
         every, early, late = range(BLOCKS), [0], [1, 2]
+        both, first, second = [0, 1], [0], [1]
 
-        def finish(a, e, tag=None):
-            quantize(a, e, tag)
-            multiply(a, e, every if e == 0 else early)
+        def finish(a, experts):
+            quantize(a, experts)
+            for e in experts:
+                multiply(a, e, every if e == 0 else early)
 
-        gather(0, [0, 1], None)
-        interleave(0, 0)
-        interleave(0, 1)
-        gather(1, [0, 1], None)
-        interleave(1, 0)
-        interleave(1, 1)
-        finish(0, 0)
-        finish(0, 1)
-        gather(2, [0, 1], "r01")
-        interleave(2, 0)
-        interleave(2, 1)
-        finish(1, 0)
-        finish(1, 1)
-        gather(3, [0], "r11")
-        interleave(3, 0)
-        finish(2, 0)
-        gather(4, [0], "r20")
-        interleave(4, 0)
-        finish(2, 1)
-        finish(3, 0)
-        gather(3, [1], "r30")
-        interleave(3, 1)
-        finish(4, 0)
-        gather(4, [1], "r40")
-        for blk in every:
-            rectify(0, blk)
-        interleave(4, 1, "first_bias")
-        for a in range(3):
-            multiply(a, 1, late)
-        quantize(3, 1)
-        multiply(3, 1, every)
+        steps = [(0, both), (1, both), (2, first), (3, first), (4, first), (2, second), (3, second), (4, second)]
+        for i, step in enumerate(steps[:-1]):
+            gather(*step, f"ring{i % 2}")
+            interleave(*step)
+            if i > 0:
+                finish(*steps[i - 1])
+            if steps[i - 1] == (PASSES - 1, first):
+                for blk in every:
+                    rectify(0, blk)
+                    square(0, blk)
+                for a in range(JOINT):
+                    multiply(a, 1, late)
+                early = every
+        gather(4, second, "ring1")
+        interleave(4, second, "first_bias")
+        finish(3, second)
         scatter(0, 0)
-        quantize(4, 1, "y00")
-        multiply(4, 1, every)
-        scatter(0, 1, "first_bias")
-        scatter(0, 2, "y01")
+        finish(4, second)
+        scatter(0, 1, "ring1")
+        scatter(0, 2, "first_bias")
         for blk in every:
             rectify(1, blk)
+            square(1, blk)
             scatter(1, blk)
             nc.sync.dma_start(out[blk * P : (blk + 1) * P, :], outs[blk][:])

@@ -27,7 +27,6 @@ HALF = 128
 HALVES = C // HALF
 SPARE = 8
 JOINT = 2
-BANKS = 8
 
 
 def tile_moe_pre_lin_relu2_kernel(tc, xT, w_words, w_scales, b, gate, offs, out):
@@ -60,25 +59,28 @@ def tile_moe_pre_lin_relu2_kernel(tc, xT, w_words, w_scales, b, gate, offs, out)
             for t in range(PACK):
                 nc.sync.dma_start(planes[a, t][:, :T], rows[a, t])
 
-        nc.sync.dma_start(offsets[:], offs)
-        nc.sync.dma_start(gates[:, :C], gate[:P, :C])
+        def load_w(e):
+            nc.sync.dma_start(w_codes[e][:].bitcast(I32), w_words[e].rearrange("a p n -> p a n").bitcast(I32))
+
         nc.sync.dma_start(planes[0, 0][:, :T], rows[0, 0])
+        nc.sync.dma_start(gates[:, :C], gate[:P, :C])
+        nc.sync.dma_start(offsets[:], offs)
         nc.sync.dma_start(gates[:, C:], gate[:P, C:])
         for t in range(1, PACK):
             nc.sync.dma_start(planes[0, t][:, :T], rows[0, t])
         load_x(1)
-        nc.sync.dma_start(bias[:], b.rearrange("(c p) e -> p c e", p=P))
         load_x(2)
+        load_x(3)
+        load_x(4)
         scale_rows = w_scales.rearrange("e a (q r) n -> r q (e a) n", r=4)
         for r in range(4):
             nc.sync.dma_start(
                 w_plane[:].bitcast(I32)[r:P:32, :].rearrange("q (g n) -> q g n", g=E * PASSES),
                 scale_rows[r].bitcast(I32),
             )
-        for e in range(E):
-            nc.sync.dma_start(w_codes[e][:].bitcast(I32), w_words[e].rearrange("a p n -> p a n").bitcast(I32))
-        load_x(3)
-        load_x(4)
+        load_w(0)
+        load_w(1)
+        nc.sync.dma_start(bias[:], b.rearrange("(c p) e -> p c e", p=P))
 
         bias0 = new([P, BLOCKS], F32, "bias0", tag="first_bias")
         nc.scalar.activation(bias0[:], bias[:, :, 0], COPY)
@@ -89,7 +91,7 @@ def tile_moe_pre_lin_relu2_kernel(tc, xT, w_words, w_scales, b, gate, offs, out)
             lo, hi = experts[0] * C, (experts[-1] + 1) * C
             g = new([P, PACK, hi - lo], F32, f"g{a}{experts[0]}", tag)
             for t in range(PACK):
-                cuts = [lo, lo + C, hi] if (a, t) == (0, 0) else [lo, hi]
+                cuts = [lo, lo + C, hi] if (a, t) in ((0, 0), (JOINT - 1, PACK - 1)) else [lo, hi]
                 for s0, s1 in zip(cuts, cuts[1:]):
                     nc.vector.tensor_tensor(
                         g[:, t, s0 - lo : s1 - lo],
@@ -102,9 +104,12 @@ def tile_moe_pre_lin_relu2_kernel(tc, xT, w_words, w_scales, b, gate, offs, out)
         def interleave(a, experts, tag=None):
             g = gathered[a, experts[0]]
             r = new([P, len(experts) * C, PACK], BF16, f"r{a}{experts[0]}", tag)
-            nc.scalar.activation(
-                r[:].rearrange("p (c i) t -> p c t i", i=4), g[:].rearrange("p t (c i) -> p c t i", i=4), COPY
-            )
+            for i in range(len(experts)):
+                nc.scalar.activation(
+                    r[:, i * C : (i + 1) * C, :].rearrange("p (c i) t -> p c t i", i=4),
+                    g[:, :, i * C : (i + 1) * C].rearrange("p t (c i) -> p c t i", i=4),
+                    COPY,
+                )
             rounded[a, experts[0]] = r
 
         def quantize(a, experts):
@@ -121,8 +126,7 @@ def tile_moe_pre_lin_relu2_kernel(tc, xT, w_words, w_scales, b, gate, offs, out)
             for blk in blocks:
                 for h in range(HALVES):
                     if a == 0:
-                        bank = ((e * BLOCKS + blk) * HALVES + h) % BANKS
-                        acc[e, blk, h] = psum.tile([P, HALF], F32, name=f"acc{e}{blk}{h}", tag=f"bank{bank}")
+                        acc[e, blk, h] = psum.tile([P, HALF], F32, name=f"acc{e}{blk}{h}", tag=f"bank{blk}{h}")
                     col = (e * PASSES + a) * N + blk * P
                     nc.tensor.matmul_mx(
                         out=acc[e, blk, h][:],
@@ -151,7 +155,7 @@ def tile_moe_pre_lin_relu2_kernel(tc, xT, w_words, w_scales, b, gate, offs, out)
                 outs[blk][:].indirect(offsets[:, e * C // 16 : (e + 1) * C // 16]), squared[e, blk][:]
             )
 
-        every, early, late = range(BLOCKS), [0], [1, 2]
+        every, early, late = range(BLOCKS), [], range(BLOCKS)
         both, first, second = [0, 1], [0], [1]
 
         def finish(a, experts):
@@ -162,7 +166,7 @@ def tile_moe_pre_lin_relu2_kernel(tc, xT, w_words, w_scales, b, gate, offs, out)
         steps = [(0, both), (1, both), (2, first), (3, first), (4, first), (2, second), (3, second), (4, second)]
         for i, step in enumerate(steps[:-1]):
             gather(*step, f"ring{i % 2}")
-            interleave(*step)
+            interleave(*step, "first_bias" if step == (3, second) else None)
             if i > 0:
                 finish(*steps[i - 1])
             if steps[i - 1] == (PASSES - 1, first):
@@ -173,12 +177,12 @@ def tile_moe_pre_lin_relu2_kernel(tc, xT, w_words, w_scales, b, gate, offs, out)
                     multiply(a, 1, late)
                 early = every
         gather(4, second, "ring1")
-        interleave(4, second, "first_bias")
+        interleave(4, second, "ring0")
         finish(3, second)
         scatter(0, 0)
         finish(4, second)
         scatter(0, 1, "ring1")
-        scatter(0, 2, "first_bias")
+        scatter(0, 2, "ring0")
         for blk in every:
             rectify(1, blk)
             square(1, blk)

@@ -17,7 +17,6 @@ FP4X4 = mybir.dt.float4_e2m1fn_x4
 MULT = mybir.AluOpType.mult
 COPY = mybir.ActivationFunctionType.Copy
 RELU = mybir.ActivationFunctionType.Relu
-SQUARE = mybir.ActivationFunctionType.Square
 
 P = 128
 PACK = 4
@@ -27,6 +26,7 @@ HALF = 128
 HALVES = C // HALF
 SPARE = 8
 JOINT = 2
+CUT = ((0, 0), (JOINT - 1, PACK - 1))
 
 
 def tile_moe_pre_lin_relu2_kernel(tc, xT, w_words, w_scales, b, gate, offs, out):
@@ -43,14 +43,15 @@ def tile_moe_pre_lin_relu2_kernel(tc, xT, w_words, w_scales, b, gate, offs, out)
         planes = {}
         for a in range(PASSES):
             for t in range(PACK):
-                planes[a, t] = new([P, T + (SPARE if a < JOINT else 0)], F32, f"x{a}{t}")
+                planes[a, t] = new([P, T + (SPARE if a < JOINT and (a, t) not in CUT else 0)], F32, f"x{a}{t}")
         w_codes = [new([P, PASSES, 2 * N], U8, f"w{e}") for e in range(E)]
         w_plane = new([P, E * PASSES * N], U8, "w_plane")
         bias = new([P, BLOCKS, E], F32, "bias")
 
         for a in range(JOINT):
             for t in range(PACK):
-                nc.vector.memset(planes[a, t][:, T:], 0.0)
+                if (a, t) not in CUT:
+                    nc.vector.memset(planes[a, t][:, T:], 0.0)
         nc.vector.memset(w_plane[:].bitcast(I32), 0)
 
         rows = xT.rearrange("(a p t) s -> a t p s", p=P, t=PACK)
@@ -85,13 +86,13 @@ def tile_moe_pre_lin_relu2_kernel(tc, xT, w_words, w_scales, b, gate, offs, out)
         bias0 = new([P, BLOCKS], F32, "bias0", tag="first_bias")
         nc.scalar.activation(bias0[:], bias[:, :, 0], COPY)
 
-        gathered, rounded, codes, scales, acc, relu, squared, outs = {}, {}, {}, {}, {}, {}, {}, {}
+        gathered, rounded, codes, scales, acc, relu, outs = {}, {}, {}, {}, {}, {}, {}
 
         def gather(a, experts, tag):
             lo, hi = experts[0] * C, (experts[-1] + 1) * C
             g = new([P, PACK, hi - lo], F32, f"g{a}{experts[0]}", tag)
             for t in range(PACK):
-                cuts = [lo, lo + C, hi] if (a, t) in ((0, 0), (JOINT - 1, PACK - 1)) else [lo, hi]
+                cuts = [lo, lo + C, hi] if (a, t) in CUT else [lo, hi]
                 for s0, s1 in zip(cuts, cuts[1:]):
                     nc.vector.tensor_tensor(
                         g[:, t, s0 - lo : s1 - lo],
@@ -144,16 +145,11 @@ def tile_moe_pre_lin_relu2_kernel(tc, xT, w_words, w_scales, b, gate, offs, out)
             for h in range(HALVES):
                 nc.scalar.activation(relu[e, blk][:, h * HALF : (h + 1) * HALF], acc[e, blk, h][:], RELU, bias=col)
 
-        def square(e, blk, tag=None):
-            squared[e, blk] = new([P, C], F32, f"z{e}{blk}", tag)
-            nc.scalar.activation(squared[e, blk][:], relu[e, blk][:], SQUARE)
-
         def scatter(e, blk, tag=None):
             if e == 0:
                 outs[blk] = new([P, T], F32, f"o{blk}", tag)
-            nc.vector.tensor_copy(
-                outs[blk][:].indirect(offsets[:, e * C // 16 : (e + 1) * C // 16]), squared[e, blk][:]
-            )
+            y = relu[e, blk][:]
+            nc.vector.tensor_tensor(outs[blk][:].indirect(offsets[:, e * C // 16 : (e + 1) * C // 16]), y, y, MULT)
 
         every, early, late = range(BLOCKS), [], range(BLOCKS)
         both, first, second = [0, 1], [0], [1]
@@ -172,7 +168,6 @@ def tile_moe_pre_lin_relu2_kernel(tc, xT, w_words, w_scales, b, gate, offs, out)
             if steps[i - 1] == (PASSES - 1, first):
                 for blk in every:
                     rectify(0, blk)
-                    square(0, blk)
                 for a in range(JOINT):
                     multiply(a, 1, late)
                 early = every
@@ -185,6 +180,5 @@ def tile_moe_pre_lin_relu2_kernel(tc, xT, w_words, w_scales, b, gate, offs, out)
         scatter(0, 2, "ring0")
         for blk in every:
             rectify(1, blk)
-            square(1, blk)
             scatter(1, blk)
             nc.sync.dma_start(out[blk * P : (blk + 1) * P, :], outs[blk][:])

@@ -4,7 +4,7 @@ import concourse.mybir as mybir
 
 K, T, E, C, N = 2560, 512, 2, 256, 384
 FLOPS = 2 * K * N * E * C
-BYTES = K * T * 4 + E * K * N // 2 + E * K // 32 * N + N * E * 4 + E * C * 4 + 128 * 32 * 2 + N * T * 4
+BYTES = K * T * 4 + E * K * N // 2 + E * K // 32 * N + N * E * 4 + E * C * 4 + E * C * 2 * 8 + N * T * 4
 
 F32 = mybir.dt.float32
 BF16 = mybir.dt.bfloat16
@@ -22,10 +22,12 @@ P = 128
 PACK = 4
 PASSES = K // (P * PACK)
 BLOCKS = N // P
-HALF = 128
-HALVES = C // HALF
+MOVING = 128
+LIST = 16
+RUN = 4
+
+JOINT = 3
 SPARE = 8
-JOINT = 2
 CUT = ((0, 0), (JOINT - 1, PACK - 1))
 
 
@@ -38,52 +40,40 @@ def tile_moe_pre_lin_relu2_kernel(tc, xT, w_words, w_scales, b, gate, offs, out)
         def new(shape, dtype, name, tag=None):
             return keep.tile(shape, dtype, name=name, tag=tag or name, align_bytes=64)
 
-        offsets = keep.tile([P, E * C // 16], U16, name="offsets")
+        whole_list = [(a, t) for a in range(JOINT) for t in range(PACK) if (a, t) not in CUT]
+
+        offsets = keep.tile([P, E * C // LIST], U16, name="offsets")
         gates = new([P, E * C], F32, "gates")
         planes = {}
         for a in range(PASSES):
             for t in range(PACK):
-                planes[a, t] = new([P, T + (SPARE if a < JOINT and (a, t) not in CUT else 0)], F32, f"x{a}{t}")
+                planes[a, t] = new([P, T + (SPARE if (a, t) in whole_list else 0)], F32, f"x{a}{t}")
         w_codes = [new([P, PASSES, 2 * N], U8, f"w{e}") for e in range(E)]
-        w_plane = new([P, E * PASSES * N], U8, "w_plane")
+        w_scale_bytes = new([P, E * PASSES * N], U8, "w_scale_bytes")
         bias = new([P, BLOCKS, E], F32, "bias")
 
-        for a in range(JOINT):
-            for t in range(PACK):
-                if (a, t) not in CUT:
-                    nc.vector.memset(planes[a, t][:, T:], 0.0)
-        nc.vector.memset(w_plane[:].bitcast(I32), 0)
+        for a, t in whole_list:
+            nc.vector.memset(planes[a, t][:, T:], 0.0)
+        nc.vector.memset(w_scale_bytes[:].bitcast(I32), 0)
 
         rows = xT.rearrange("(a p t) s -> a t p s", p=P, t=PACK)
-
-        def load_x(a):
-            for t in range(PACK):
-                nc.sync.dma_start(planes[a, t][:, :T], rows[a, t])
-
-        def load_w(e):
-            nc.sync.dma_start(w_codes[e][:].bitcast(I32), w_words[e].rearrange("a p n -> p a n").bitcast(I32))
-
         nc.sync.dma_start(planes[0, 0][:, :T], rows[0, 0])
         nc.sync.dma_start(gates[:, :C], gate[:P, :C])
         nc.sync.dma_start(offsets[:], offs)
         nc.sync.dma_start(gates[:, C:], gate[:P, C:])
-        for t in range(1, PACK):
-            nc.sync.dma_start(planes[0, t][:, :T], rows[0, t])
-        load_x(1)
-        load_x(2)
-        load_x(3)
-        load_x(4)
-        scale_rows = w_scales.rearrange("e a (q r) n -> r q (e a) n", r=4)
+        for a, t in list(planes)[1:]:
+            nc.sync.dma_start(planes[a, t][:, :T], rows[a, t])
+        scale_rows = w_scales.rearrange("e a (u r) n -> r u (e a) n", r=4)
         for r in range(4):
             nc.sync.dma_start(
-                w_plane[:].bitcast(I32)[r:P:32, :].rearrange("q (g n) -> q g n", g=E * PASSES),
+                w_scale_bytes[:].bitcast(I32)[r:P:32, :].rearrange("u (g n) -> u g n", g=E * PASSES),
                 scale_rows[r].bitcast(I32),
             )
-        load_w(0)
-        load_w(1)
+        for e in range(E):
+            nc.sync.dma_start(w_codes[e][:].bitcast(I32), w_words[e].rearrange("a p n -> p a n").bitcast(I32))
         nc.sync.dma_start(bias[:], b.rearrange("(c p) e -> p c e", p=P))
 
-        bias0 = new([P, BLOCKS], F32, "bias0", tag="first_bias")
+        bias0 = new([P, BLOCKS], F32, "bias0", tag="after_relu0")
         nc.scalar.activation(bias0[:], bias[:, :, 0], COPY)
 
         gathered, rounded, codes, scales, acc, relu, outs = {}, {}, {}, {}, {}, {}, {}
@@ -96,7 +86,7 @@ def tile_moe_pre_lin_relu2_kernel(tc, xT, w_words, w_scales, b, gate, offs, out)
                 for s0, s1 in zip(cuts, cuts[1:]):
                     nc.vector.tensor_tensor(
                         g[:, t, s0 - lo : s1 - lo],
-                        planes[a, t][:].indirect(offsets[:, s0 // 16 : s1 // 16]),
+                        planes[a, t][:].indirect(offsets[:, s0 // LIST : s1 // LIST]),
                         gates[:, s0:s1],
                         MULT,
                     )
@@ -107,8 +97,8 @@ def tile_moe_pre_lin_relu2_kernel(tc, xT, w_words, w_scales, b, gate, offs, out)
             r = new([P, len(experts) * C, PACK], BF16, f"r{a}{experts[0]}", tag)
             for i in range(len(experts)):
                 nc.scalar.activation(
-                    r[:, i * C : (i + 1) * C, :].rearrange("p (c i) t -> p c t i", i=4),
-                    g[:, :, i * C : (i + 1) * C].rearrange("p t (c i) -> p c t i", i=4),
+                    r[:, i * C : (i + 1) * C, :].rearrange("p (c i) t -> p c t i", i=RUN),
+                    g[:, :, i * C : (i + 1) * C].rearrange("p t (c i) -> p c t i", i=RUN),
                     COPY,
                 )
             rounded[a, experts[0]] = r
@@ -123,18 +113,18 @@ def tile_moe_pre_lin_relu2_kernel(tc, xT, w_words, w_scales, b, gate, offs, out)
                 codes[a, e] = c[:, i * C : (i + 1) * C]
                 scales[a, e] = s[:, i * C : (i + 1) * C]
 
-        def multiply(a, e, blocks):
-            for blk in blocks:
-                for h in range(HALVES):
+        def multiply(a, e):
+            for blk in range(BLOCKS):
+                for h in range(C // MOVING):
                     if a == 0:
-                        acc[e, blk, h] = psum.tile([P, HALF], F32, name=f"acc{e}{blk}{h}", tag=f"bank{blk}{h}")
+                        acc[e, blk, h] = psum.tile([P, MOVING], F32, name=f"acc{e}{blk}{h}", tag=f"bank{blk}{h}")
                     col = (e * PASSES + a) * N + blk * P
                     nc.tensor.matmul_mx(
                         out=acc[e, blk, h][:],
                         lhsT=w_codes[e][:, a, 2 * blk * P : 2 * (blk + 1) * P].bitcast(FP4X4),
-                        lhsT_scale=w_plane[:, col : col + P],
-                        rhs=codes[a, e][:, h * HALF : (h + 1) * HALF].bitcast(FP8X4),
-                        rhs_scale=scales[a, e][:, h * HALF : (h + 1) * HALF],
+                        lhsT_scale=w_scale_bytes[:, col : col + P],
+                        rhs=codes[a, e][:, h * MOVING : (h + 1) * MOVING].bitcast(FP8X4),
+                        rhs_scale=scales[a, e][:, h * MOVING : (h + 1) * MOVING],
                         start=(a == 0),
                         stop=(a == PASSES - 1),
                     )
@@ -142,43 +132,39 @@ def tile_moe_pre_lin_relu2_kernel(tc, xT, w_words, w_scales, b, gate, offs, out)
         def rectify(e, blk):
             relu[e, blk] = new([P, C], F32, f"y{e}{blk}")
             col = bias0[:, blk : blk + 1] if e == 0 else bias[:, blk, 1:2]
-            for h in range(HALVES):
-                nc.scalar.activation(relu[e, blk][:, h * HALF : (h + 1) * HALF], acc[e, blk, h][:], RELU, bias=col)
+            for h in range(C // MOVING):
+                nc.scalar.activation(relu[e, blk][:, h * MOVING : (h + 1) * MOVING], acc[e, blk, h][:], RELU, bias=col)
 
         def scatter(e, blk, tag=None):
             if e == 0:
                 outs[blk] = new([P, T], F32, f"o{blk}", tag)
             y = relu[e, blk][:]
-            nc.vector.tensor_tensor(outs[blk][:].indirect(offsets[:, e * C // 16 : (e + 1) * C // 16]), y, y, MULT)
+            nc.vector.tensor_tensor(outs[blk][:].indirect(offsets[:, e * C // LIST : (e + 1) * C // LIST]), y, y, MULT)
 
-        every, early, late = range(BLOCKS), [], range(BLOCKS)
-        both, first, second = [0, 1], [0], [1]
-
-        def finish(a, experts):
-            quantize(a, experts)
-            for e in experts:
-                multiply(a, e, every if e == 0 else early)
-
-        steps = [(0, both), (1, both), (2, first), (3, first), (4, first), (2, second), (3, second), (4, second)]
+        split = range(JOINT, PASSES)
+        steps = [(a, [0, 1]) for a in range(JOINT)] + [(a, [0]) for a in split] + [(a, [1]) for a in split]
+        buffers = [f"gathered{i % 2}" for i in range(len(steps))]
         for i, step in enumerate(steps[:-1]):
-            gather(*step, f"ring{i % 2}")
-            interleave(*step, "first_bias" if step == (3, second) else None)
+            gather(*step, buffers[i])
+            interleave(*step)
             if i > 0:
-                finish(*steps[i - 1])
-            if steps[i - 1] == (PASSES - 1, first):
-                for blk in every:
-                    rectify(0, blk)
-                for a in range(JOINT):
-                    multiply(a, 1, late)
-                early = every
-        gather(4, second, "ring1")
-        interleave(4, second, "ring0")
-        finish(3, second)
+                quantize(*steps[i - 1])
+                multiply(steps[i - 1][0], 0)
+        for blk in range(BLOCKS):
+            rectify(0, blk)
+        for a in range(JOINT):
+            multiply(a, 1)
+
+        gather(*steps[-1], buffers[-1])
+        interleave(*steps[-1], "after_relu0")
+        quantize(*steps[-2])
+        multiply(PASSES - 2, 1)
         scatter(0, 0)
-        finish(4, second)
-        scatter(0, 1, "ring1")
-        scatter(0, 2, "ring0")
-        for blk in every:
+        quantize(*steps[-1])
+        multiply(PASSES - 1, 1)
+        scatter(0, 1, buffers[-1])
+        scatter(0, 2, "after_relu0")
+        for blk in range(BLOCKS):
             rectify(1, blk)
             scatter(1, blk)
             nc.sync.dma_start(out[blk * P : (blk + 1) * P, :], outs[blk][:])

from contextlib import ExitStack

import concourse.mybir as mybir

K, T, E, C, N = 2560, 512, 2, 256, 384
FLOPS = 2 * K * N * E * C
BYTES = K * T * 4 + E * K * N // 2 + E * K // 32 * N + N * E * 4 + E * C * 4 + E * C * 2 * 8 + N * T * 4

F32 = mybir.dt.float32
BF16 = mybir.dt.bfloat16
I32 = mybir.dt.int32
U32 = mybir.dt.uint32
U16 = mybir.dt.uint16
U8 = mybir.dt.uint8
FP8X4 = mybir.dt.float8_e4m3fn_x4
FP4X4 = mybir.dt.float4_e2m1fn_x4
MULT = mybir.AluOpType.mult
COPY = mybir.ActivationFunctionType.Copy
RELU = mybir.ActivationFunctionType.Relu

P = 128
PACK = 4
PASSES = K // (P * PACK)
BLOCKS = N // P
MOVING = 128
LIST = 16
RUN = 4

JOINT = 3
SPARE = 8
CUT = ((0, 0), (JOINT - 1, PACK - 1))


def tile_moe_pre_lin_relu2_kernel(tc, xT, w_words, w_scales, b, gate, offs, out):
    nc = tc.nc
    with ExitStack() as ctx:
        keep = ctx.enter_context(tc.tile_pool(name="keep", bufs=1))
        psum = ctx.enter_context(tc.psum_pool(name="psum", bufs=1))

        def new(shape, dtype, name, tag=None):
            return keep.tile(shape, dtype, name=name, tag=tag or name, align_bytes=64)

        whole_list = [(a, t) for a in range(JOINT) for t in range(PACK) if (a, t) not in CUT]

        offsets = keep.tile([P, E * C // LIST], U16, name="offsets")
        gates = new([P, E * C], F32, "gates")
        planes = {}
        for a in range(PASSES):
            for t in range(PACK):
                planes[a, t] = new([P, T + (SPARE if (a, t) in whole_list else 0)], F32, f"x{a}{t}")
        w_codes = [new([P, PASSES, 2 * N], U8, f"w{e}") for e in range(E)]
        w_scale_bytes = new([P, E * PASSES * N], U8, "w_scale_bytes")
        bias = new([P, BLOCKS, E], F32, "bias")

        for a, t in whole_list:
            nc.vector.memset(planes[a, t][:, T:], 0.0)
        nc.vector.memset(w_scale_bytes[:].bitcast(I32), 0)

        rows = xT.rearrange("(a p t) s -> a t p s", p=P, t=PACK)
        nc.sync.dma_start(planes[0, 0][:, :T], rows[0, 0])
        nc.sync.dma_start(gates[:, :C], gate[:P, :C])
        nc.sync.dma_start(offsets[:], offs)
        nc.sync.dma_start(gates[:, C:], gate[:P, C:])
        for a, t in list(planes)[1:]:
            nc.sync.dma_start(planes[a, t][:, :T], rows[a, t])
        scale_rows = w_scales.rearrange("e a (u r) n -> r u (e a) n", r=4)
        for r in range(4):
            nc.sync.dma_start(
                w_scale_bytes[:].bitcast(I32)[r:P:32, :].rearrange("u (g n) -> u g n", g=E * PASSES),
                scale_rows[r].bitcast(I32),
            )
        for e in range(E):
            nc.sync.dma_start(w_codes[e][:].bitcast(I32), w_words[e].rearrange("a p n -> p a n").bitcast(I32))
        nc.sync.dma_start(bias[:], b.rearrange("(c p) e -> p c e", p=P))

        bias0 = new([P, BLOCKS], F32, "bias0", tag="after_relu0")
        nc.scalar.activation(bias0[:], bias[:, :, 0], COPY)

        gathered, rounded, codes, scales, acc, relu, outs = {}, {}, {}, {}, {}, {}, {}

        def gather(a, experts, tag):
            lo, hi = experts[0] * C, (experts[-1] + 1) * C
            g = new([P, PACK, hi - lo], F32, f"g{a}{experts[0]}", tag)
            for t in range(PACK):
                cuts = [lo, lo + C, hi] if (a, t) in CUT else [lo, hi]
                for s0, s1 in zip(cuts, cuts[1:]):
                    nc.vector.tensor_tensor(
                        g[:, t, s0 - lo : s1 - lo],
                        planes[a, t][:].indirect(offsets[:, s0 // LIST : s1 // LIST]),
                        gates[:, s0:s1],
                        MULT,
                    )
            gathered[a, experts[0]] = g

        def interleave(a, experts, tag=None):
            g = gathered[a, experts[0]]
            r = new([P, len(experts) * C, PACK], BF16, f"r{a}{experts[0]}", tag)
            for i in range(len(experts)):
                nc.scalar.activation(
                    r[:, i * C : (i + 1) * C, :].rearrange("p (c i) t -> p c t i", i=RUN),
                    g[:, :, i * C : (i + 1) * C].rearrange("p t (c i) -> p c t i", i=RUN),
                    COPY,
                )
            rounded[a, experts[0]] = r

        def quantize(a, experts):
            c = new([P, len(experts) * C], U32, f"c{a}{experts[0]}")
            s = new([P, len(experts) * C], U8, f"s{a}{experts[0]}")
            nc.vector.quantize_mx(
                out=c[:].bitcast(FP8X4), scales=s[:], in_=rounded[a, experts[0]][:].rearrange("p c t -> p (c t)")
            )
            for i, e in enumerate(experts):
                codes[a, e] = c[:, i * C : (i + 1) * C]
                scales[a, e] = s[:, i * C : (i + 1) * C]

        def multiply(a, e):
            for blk in range(BLOCKS):
                for h in range(C // MOVING):
                    if a == 0:
                        acc[e, blk, h] = psum.tile([P, MOVING], F32, name=f"acc{e}{blk}{h}", tag=f"bank{blk}{h}")
                    col = (e * PASSES + a) * N + blk * P
                    nc.tensor.matmul_mx(
                        out=acc[e, blk, h][:],
                        lhsT=w_codes[e][:, a, 2 * blk * P : 2 * (blk + 1) * P].bitcast(FP4X4),
                        lhsT_scale=w_scale_bytes[:, col : col + P],
                        rhs=codes[a, e][:, h * MOVING : (h + 1) * MOVING].bitcast(FP8X4),
                        rhs_scale=scales[a, e][:, h * MOVING : (h + 1) * MOVING],
                        start=(a == 0),
                        stop=(a == PASSES - 1),
                    )

        def rectify(e, blk):
            relu[e, blk] = new([P, C], F32, f"y{e}{blk}")
            col = bias0[:, blk : blk + 1] if e == 0 else bias[:, blk, 1:2]
            for h in range(C // MOVING):
                nc.scalar.activation(relu[e, blk][:, h * MOVING : (h + 1) * MOVING], acc[e, blk, h][:], RELU, bias=col)

        def scatter(e, blk, tag=None):
            if e == 0:
                outs[blk] = new([P, T], F32, f"o{blk}", tag)
            y = relu[e, blk][:]
            nc.vector.tensor_tensor(outs[blk][:].indirect(offsets[:, e * C // LIST : (e + 1) * C // LIST]), y, y, MULT)

        split = range(JOINT, PASSES)
        steps = [(a, [0, 1]) for a in range(JOINT)] + [(a, [0]) for a in split] + [(a, [1]) for a in split]
        buffers = [f"gathered{i % 2}" for i in range(len(steps))]
        for i, step in enumerate(steps[:-1]):
            gather(*step, buffers[i])
            interleave(*step)
            if i > 0:
                quantize(*steps[i - 1])
                multiply(steps[i - 1][0], 0)
        for blk in range(BLOCKS):
            rectify(0, blk)
        for a in range(JOINT):
            multiply(a, 1)

        gather(*steps[-1], buffers[-1])
        interleave(*steps[-1], "after_relu0")
        quantize(*steps[-2])
        multiply(PASSES - 2, 1)
        scatter(0, 0)
        quantize(*steps[-1])
        multiply(PASSES - 1, 1)
        scatter(0, 1, buffers[-1])
        scatter(0, 2, "after_relu0")
        for blk in range(BLOCKS):
            rectify(1, blk)
            scatter(1, blk)
            nc.sync.dma_start(out[blk * P : (blk + 1) * P, :], outs[blk][:])
